import numpy as np
import ml_dtypes


def mxq(x, axis, fmt="e4m3"):
    dtype, down = {"e4m3": (ml_dtypes.float8_e4m3fn, 7), "e5m2": (ml_dtypes.float8_e5m2, 14)}[fmt]
    v = np.moveaxis(np.asarray(x, np.float32).astype(ml_dtypes.bfloat16).astype(np.float64), axis, -1)
    blocks = v.reshape(v.shape[:-1] + (-1, 32))
    amax = np.abs(blocks).max(-1, keepdims=True)
    byte = np.maximum(np.where(amax > 0, np.frexp(amax)[1] - 1 + 127, 0) - down, 1)
    scale = np.exp2(byte - 127.0)
    codes = (blocks / scale).astype(np.float32).astype(dtype).astype(np.float64)
    return np.moveaxis((codes * scale).reshape(v.shape), -1, axis)


WIDE = False


def mx_kscale(k):
    if not WIDE:
        return np.ones(k)
    levels = np.array([10, -10, 5, -5, 0])
    if k % 512:
        return np.exp2(np.random.permutation(np.resize(levels, k // 32))).repeat(32)
    a = np.empty((k // 512, 16))
    for p in range(k // 512):
        a[p, :8] = np.random.permutation(np.resize(levels, 8))
        for g in range(8):
            far = levels[np.abs(levels - a[p, g]) >= 10]
            a[p, g + 8] = far[np.random.randint(len(far))]
    return np.exp2(a.ravel()).repeat(32)


def f64(x):
    return np.asarray(x).astype(np.float64)


def striped8(idx):
    return np.concatenate([v.reshape(-1, 16).T for v in idx]).astype(np.uint16)


def unstriped8(offs):
    return np.stack([offs[16 * g:16 * g + 16].T.reshape(-1) for g in range(8)]).astype(np.int64)


E2M1 = np.array([0.0, 0.5, 1.0, 1.5, 2.0, 3.0, 4.0, 6.0, -0.0, -0.5, -1.0, -1.5, -2.0, -3.0, -4.0, -6.0])


def pack_weight(w, fmt):
    k, n = w.shape
    w = f64(np.asarray(w, np.float32).astype(ml_dtypes.bfloat16)).reshape(k // 32, 32, n)
    amax = np.abs(w).max(1)
    if fmt == "e4m3":
        byte = np.frexp(amax)[1] - 1 + 127 - 7
    else:
        mant, ex = np.frexp(amax / 6.0)
        byte = np.where(mant > 0.5, ex, ex - 1) + 127
    byte = np.clip(np.where(amax > 0, byte, 1), 1, 254)
    scaled = (w * np.exp2(127.0 - byte)[:, None, :]).reshape(k, n).astype(np.float32)
    by_word = np.ascontiguousarray(scaled.reshape(k // 512, 128, 4, n).transpose(0, 1, 3, 2))
    if fmt == "e4m3":
        words = by_word.astype(ml_dtypes.float8_e4m3fn).view(np.uint8)
    else:
        c = by_word.astype(ml_dtypes.float4_e2m1fn).view(np.uint8) & 0xF
        words = (c[..., 0::2] | (c[..., 1::2] << 4)).reshape(k // 512, 128, 2 * n)
    return np.ascontiguousarray(words), np.ascontiguousarray(byte.astype(np.uint8).reshape(k // 512, 16, n))


def unpack_weight(words, scales, fmt):
    g, _, n = scales.shape
    words = np.ascontiguousarray(words).reshape(g, 128, n, -1)
    if fmt == "e4m3":
        vals = words.view(ml_dtypes.float8_e4m3fn).astype(np.float64)
    else:
        nib = np.empty((g, 128, n, 4), np.uint8)
        nib[..., 0::2] = words & 0xF
        nib[..., 1::2] = words >> 4
        vals = E2M1[nib]
    vals = vals * np.repeat(np.exp2(scales.astype(np.float64) - 127.0), 8, axis=1)[..., None]
    return vals.transpose(0, 1, 3, 2).reshape(g * 512, n)


K, M, T, S = 512, 512, 2048, 1024


def setup_inputs():
    n = np.random.standard_normal
    s = mx_kscale(K)[:, None]
    p_w = pack_weight(n((K, M)) / np.sqrt(K) / s, "e2m1")
    return {
        "x": (n((K, S)) * s).astype(np.float32),
        "w_words": p_w[0],
        "w_scales": p_w[1],
        "wgo": np.repeat(np.random.uniform(0.5, 2.0, (8, S)), 16, axis=0).astype(np.float32),
        "offs": striped8(np.stack([np.random.permutation(T)[:S] for _ in range(8)])),
    }


def reference(x, w_words, w_scales, wgo, offs):
    x_ = mxq(f64(x), 0, "e4m3")
    w_ = unpack_weight(w_words, w_scales, "e2m1")
    y = w_.T @ x_
    place = unstriped8(offs)[np.arange(M) % 128 // 16]
    out = np.zeros((M, T))
    out[np.arange(M)[:, None], place] = f64(wgo)[np.arange(M) % 128] * (y)
    return out

@@ -1,0 +1,133 @@
+from contextlib import ExitStack
+
+import concourse.mybir as mybir
+
+K, M, T, S = 512, 512, 2048, 1024
+FLOPS = 2 * K * M * S
+
+F32 = mybir.dt.float32
+BF16 = mybir.dt.bfloat16
+I32 = mybir.dt.int32
+U32 = mybir.dt.uint32
+U16 = mybir.dt.uint16
+U8 = mybir.dt.uint8
+FP8X4 = mybir.dt.float8_e4m3fn_x4
+FP4X4 = mybir.dt.float4_e2m1fn_x4
+
+P = 128
+PACK = 4
+HALF = 512
+CHUNK = 256
+BLOCKS = M // P
+LIST_COLS = HALF // 16
+VECTOR_COLS = 160
+
+
+def tile_list_hscat_none_kernel(tc, x, w_words, w_scales, wgo, offs, out):
+    nc = tc.nc
+    mult = mybir.AluOpType.mult
+    x_rows = x.rearrange("(p j) s -> p j s", j=PACK)
+
+    with ExitStack() as ctx:
+        keep = ctx.enter_context(tc.tile_pool(name="keep", bufs=1))
+        windows = ctx.enter_context(tc.tile_pool(name="windows", bufs=3))
+        psum = ctx.enter_context(tc.psum_pool(name="psum", bufs=1))
+
+        offsets = keep.tile([P, S // 16], U16, name="offsets")
+        words = keep.tile([P, 2 * M], U8, name="words", align_bytes=64)
+        w_plane = keep.tile([P, M], U8, name="w_plane", align_bytes=64)
+        weights = [keep.tile([P, HALF], F32, name=f"weights{h}") for h in range(2)]
+        raw_a = [keep.tile([P, PACK, CHUNK], F32, name=f"raw_a{c}") for c in range(2)]
+        raw_b = keep.tile([P, PACK, HALF], F32, name="raw_b")
+        grouped_a = [keep.tile([P, CHUNK, PACK], BF16, name=f"grouped_a{c}", align_bytes=64) for c in range(2)]
+        grouped_b = keep.tile([P, HALF, PACK], BF16, name="grouped_b", align_bytes=64)
+        codes = [keep.tile([P, HALF], U32, name=f"codes{h}", align_bytes=64) for h in range(2)]
+        x_plane = [keep.tile([P, HALF], U8, name=f"x_plane{h}", align_bytes=64) for h in range(2)]
+        result = [[keep.tile([P, HALF], F32, name=f"result{b}{h}") for h in range(2)] for b in range(BLOCKS)]
+        bank = [[psum.tile([P, HALF], F32, name=f"bank{b}{h}") for h in range(2)] for b in range(BLOCKS)]
+
+        nc.gpsimd.memset(w_plane[:].bitcast(I32), 0)
+        nc.sync.dma_start(out=raw_a[0][:], in_=x_rows[:, :, 0:CHUNK])
+        nc.sync.dma_start(out=raw_a[1][:], in_=x_rows[:, :, CHUNK : 2 * CHUNK])
+        nc.scalar.dma_start(out=words[:].bitcast(I32), in_=w_words[0].bitcast(I32))
+        for q in range(4):
+            nc.scalar.dma_start(
+                out=w_plane[32 * q : 32 * q + 4, :].bitcast(I32),
+                in_=w_scales[0, 4 * q : 4 * q + 4, :].bitcast(I32),
+            )
+        nc.sync.dma_start(offsets[:], offs)
+        nc.sync.dma_start(out=weights[0][:], in_=wgo[:, 0:HALF])
+        nc.sync.dma_start(out=raw_b[:], in_=x_rows[:, :, HALF:S])
+        nc.sync.dma_start(out=weights[1][:], in_=wgo[:, HALF:S])
+
+        window = {}
+
+        def clear(b, engine):
+            window[b] = windows.tile([P, T], F32, name="window")
+            engine.memset(window[b][:], 0.0)
+
+        def group(engine_copy, dst, src, c0, c1):
+            engine_copy(out=dst[:, c0:c1, :], in_=src[:, :, c0:c1].rearrange("p j c -> p c j"))
+
+        def quantize(grouped, h, c0, c1):
+            nc.vector.quantize_mx(
+                out=codes[h][:, c0:c1].bitcast(FP8X4),
+                scales=x_plane[h][:, c0:c1],
+                in_=grouped[:].rearrange("p c j -> p (c j)"),
+            )
+
+        def multiply(b, h, c0, c1):
+            nc.tensor.matmul_mx(
+                out=bank[b][h][:, c0:c1],
+                lhsT=words[:, 2 * P * b : 2 * P * (b + 1)].bitcast(FP4X4),
+                lhsT_scale=w_plane[:, P * b : P * (b + 1)],
+                rhs=codes[h][:, c0:c1].bitcast(FP8X4),
+                rhs_scale=x_plane[h][:, c0:c1],
+                start=True,
+                stop=True,
+            )
+            nc.scalar.copy(out=result[b][h][:, c0:c1], in_=bank[b][h][:, c0:c1])
+
+        def place(b, h):
+            nc.vector.tensor_tensor(
+                window[b][:].indirect(offsets[:, LIST_COLS * h : LIST_COLS * (h + 1)]),
+                result[b][h][:],
+                weights[h][:],
+                mult,
+            )
+
+        def store(b):
+            nc.sync.dma_start(out=out[P * b : P * (b + 1), :], in_=window[b][:])
+
+        for b in range(3):
+            clear(b, nc.vector)
+
+        group(nc.vector.tensor_copy, grouped_a[0], raw_a[0], 0, CHUNK)
+        quantize(grouped_a[0], 0, 0, CHUNK)
+        multiply(0, 0, 0, CHUNK)
+        group(nc.vector.tensor_copy, grouped_a[1], raw_a[1], 0, VECTOR_COLS)
+        group(nc.scalar.copy, grouped_a[1], raw_a[1], VECTOR_COLS, CHUNK)
+        quantize(grouped_a[1], 0, CHUNK, HALF)
+        multiply(0, 0, CHUNK, HALF)
+        multiply(1, 0, 0, HALF)
+        place(0, 0)
+        group(nc.scalar.copy, grouped_b, raw_b, 0, HALF)
+        place(1, 0)
+        quantize(grouped_b, 1, 0, HALF)
+        multiply(0, 1, 0, HALF)
+        multiply(2, 0, 0, HALF)
+        multiply(1, 1, 0, HALF)
+        multiply(2, 1, 0, HALF)
+        multiply(3, 0, 0, HALF)
+        multiply(3, 1, 0, HALF)
+        place(0, 1)
+        store(0)
+        place(2, 0)
+        place(1, 1)
+        store(1)
+        clear(3, nc.gpsimd)
+        place(3, 0)
+        place(2, 1)
+        store(2)
+        place(3, 1)
+        store(3)

@@ -30,7 +30,7 @@ def tile_list_hscat_none_kernel(tc, x, w_words, w_scales, wgo, offs, out):
 
     with ExitStack() as ctx:
         keep = ctx.enter_context(tc.tile_pool(name="keep", bufs=1))
-        windows = ctx.enter_context(tc.tile_pool(name="windows", bufs=3))
+        windows = ctx.enter_context(tc.tile_pool(name="windows", bufs=4))
         psum = ctx.enter_context(tc.psum_pool(name="psum", bufs=1))
 
         offsets = keep.tile([P, S // 16], U16, name="offsets")
@@ -39,8 +39,7 @@ def tile_list_hscat_none_kernel(tc, x, w_words, w_scales, wgo, offs, out):
         weights = [keep.tile([P, HALF], F32, name=f"weights{h}") for h in range(2)]
         raw_a = [keep.tile([P, PACK, CHUNK], F32, name=f"raw_a{c}") for c in range(2)]
         raw_b = keep.tile([P, PACK, HALF], F32, name="raw_b")
-        grouped_a = [keep.tile([P, CHUNK, PACK], BF16, name=f"grouped_a{c}", align_bytes=64) for c in range(2)]
-        grouped_b = keep.tile([P, HALF, PACK], BF16, name="grouped_b", align_bytes=64)
+        grouped = [windows.tile([P, HALF, PACK], BF16, name=f"grouped{h}", tag="window", align_bytes=64) for h in range(2)]
         codes = [keep.tile([P, HALF], U32, name=f"codes{h}", align_bytes=64) for h in range(2)]
         x_plane = [keep.tile([P, HALF], U8, name=f"x_plane{h}", align_bytes=64) for h in range(2)]
         result = [[keep.tile([P, HALF], F32, name=f"result{b}{h}") for h in range(2)] for b in range(BLOCKS)]
@@ -63,17 +62,17 @@ def tile_list_hscat_none_kernel(tc, x, w_words, w_scales, wgo, offs, out):
         window = {}
 
         def clear(b, engine):
-            window[b] = windows.tile([P, T], F32, name="window")
+            window[b] = windows.tile([P, T], F32, name=f"window{b}", tag="window", align_bytes=64)
             engine.memset(window[b][:], 0.0)
 
-        def group(engine_copy, dst, src, c0, c1):
-            engine_copy(out=dst[:, c0:c1, :], in_=src[:, :, c0:c1].rearrange("p j c -> p c j"))
+        def group(engine_copy, h, src, first, c0, c1):
+            engine_copy(out=grouped[h][:, c0:c1, :], in_=src[:, :, c0 - first : c1 - first].rearrange("p j c -> p c j"))
 
-        def quantize(grouped, h, c0, c1):
+        def quantize(h, c0, c1):
             nc.vector.quantize_mx(
                 out=codes[h][:, c0:c1].bitcast(FP8X4),
                 scales=x_plane[h][:, c0:c1],
-                in_=grouped[:].rearrange("p c j -> p (c j)"),
+                in_=grouped[h][:, c0:c1, :].rearrange("p c j -> p (c j)"),
             )
 
         def multiply(b, h, c0, c1):
@@ -99,21 +98,23 @@ def tile_list_hscat_none_kernel(tc, x, w_words, w_scales, wgo, offs, out):
         def store(b):
             nc.sync.dma_start(out=out[P * b : P * (b + 1), :], in_=window[b][:])
 
-        for b in range(3):
-            clear(b, nc.vector)
+        clear(0, nc.vector)
+        clear(1, nc.gpsimd)
 
-        group(nc.vector.tensor_copy, grouped_a[0], raw_a[0], 0, CHUNK)
-        quantize(grouped_a[0], 0, 0, CHUNK)
+        group(nc.vector.tensor_copy, 0, raw_a[0], 0, 0, CHUNK)
+        quantize(0, 0, CHUNK)
+        group(nc.vector.tensor_copy, 0, raw_a[1], CHUNK, CHUNK, CHUNK + VECTOR_COLS)
+        group(nc.scalar.copy, 0, raw_a[1], CHUNK, CHUNK + VECTOR_COLS, HALF)
         multiply(0, 0, 0, CHUNK)
-        group(nc.vector.tensor_copy, grouped_a[1], raw_a[1], 0, VECTOR_COLS)
-        group(nc.scalar.copy, grouped_a[1], raw_a[1], VECTOR_COLS, CHUNK)
-        quantize(grouped_a[1], 0, CHUNK, HALF)
+        quantize(0, CHUNK, HALF)
         multiply(0, 0, CHUNK, HALF)
         multiply(1, 0, 0, HALF)
         place(0, 0)
-        group(nc.scalar.copy, grouped_b, raw_b, 0, HALF)
+        clear(2, nc.gpsimd)
+        group(nc.scalar.copy, 1, raw_b, 0, 0, HALF)
         place(1, 0)
-        quantize(grouped_b, 1, 0, HALF)
+        quantize(1, 0, HALF)
+        clear(3, nc.gpsimd)
         multiply(0, 1, 0, HALF)
         multiply(2, 0, 0, HALF)
         multiply(1, 1, 0, HALF)
@@ -125,7 +126,6 @@ def tile_list_hscat_none_kernel(tc, x, w_words, w_scales, wgo, offs, out):
         place(2, 0)
         place(1, 1)
         store(1)
-        clear(3, nc.gpsimd)
         place(3, 0)
         place(2, 1)
         store(2)

@@ -30,7 +30,7 @@ def tile_list_hscat_none_kernel(tc, x, w_words, w_scales, wgo, offs, out):
 
     with ExitStack() as ctx:
         keep = ctx.enter_context(tc.tile_pool(name="keep", bufs=1))
-        windows = ctx.enter_context(tc.tile_pool(name="windows", bufs=4))
+        windows = ctx.enter_context(tc.tile_pool(name="windows", bufs=3))
         psum = ctx.enter_context(tc.psum_pool(name="psum", bufs=1))
 
         offsets = keep.tile([P, S // 16], U16, name="offsets")
@@ -39,7 +39,10 @@ def tile_list_hscat_none_kernel(tc, x, w_words, w_scales, wgo, offs, out):
         weights = [keep.tile([P, HALF], F32, name=f"weights{h}") for h in range(2)]
         raw_a = [keep.tile([P, PACK, CHUNK], F32, name=f"raw_a{c}") for c in range(2)]
         raw_b = keep.tile([P, PACK, HALF], F32, name="raw_b")
-        grouped = [windows.tile([P, HALF, PACK], BF16, name=f"grouped{h}", tag="window", align_bytes=64) for h in range(2)]
+        grouped = [
+            windows.tile([P, HALF, PACK], BF16, name="grouped0", tag="window", align_bytes=64),
+            keep.tile([P, HALF, PACK], BF16, name="grouped1", align_bytes=64),
+        ]
         codes = [keep.tile([P, HALF], U32, name=f"codes{h}", align_bytes=64) for h in range(2)]
         x_plane = [keep.tile([P, HALF], U8, name=f"x_plane{h}", align_bytes=64) for h in range(2)]
         result = [[keep.tile([P, HALF], F32, name=f"result{b}{h}") for h in range(2)] for b in range(BLOCKS)]
@@ -61,9 +64,9 @@ def tile_list_hscat_none_kernel(tc, x, w_words, w_scales, wgo, offs, out):
 
         window = {}
 
-        def clear(b, engine):
+        def clear(b):
             window[b] = windows.tile([P, T], F32, name=f"window{b}", tag="window", align_bytes=64)
-            engine.memset(window[b][:], 0.0)
+            nc.vector.memset(window[b][:], 0.0)
 
         def group(engine_copy, h, src, first, c0, c1):
             engine_copy(out=grouped[h][:, c0:c1, :], in_=src[:, :, c0 - first : c1 - first].rearrange("p j c -> p c j"))
@@ -98,8 +101,8 @@ def tile_list_hscat_none_kernel(tc, x, w_words, w_scales, wgo, offs, out):
         def store(b):
             nc.sync.dma_start(out=out[P * b : P * (b + 1), :], in_=window[b][:])
 
-        clear(0, nc.vector)
-        clear(1, nc.gpsimd)
+        clear(0)
+        clear(1)
 
         group(nc.vector.tensor_copy, 0, raw_a[0], 0, 0, CHUNK)
         quantize(0, 0, CHUNK)
@@ -109,12 +112,11 @@ def tile_list_hscat_none_kernel(tc, x, w_words, w_scales, wgo, offs, out):
         quantize(0, CHUNK, HALF)
         multiply(0, 0, CHUNK, HALF)
         multiply(1, 0, 0, HALF)
+        clear(2)
         place(0, 0)
-        clear(2, nc.gpsimd)
         group(nc.scalar.copy, 1, raw_b, 0, 0, HALF)
         place(1, 0)
         quantize(1, 0, HALF)
-        clear(3, nc.gpsimd)
         multiply(0, 1, 0, HALF)
         multiply(2, 0, 0, HALF)
         multiply(1, 1, 0, HALF)
@@ -126,6 +128,7 @@ def tile_list_hscat_none_kernel(tc, x, w_words, w_scales, wgo, offs, out):
         place(2, 0)
         place(1, 1)
         store(1)
+        window[3] = window[0]
         place(3, 0)
         place(2, 1)
         store(2)

@@ -40,7 +40,7 @@ def tile_list_hscat_none_kernel(tc, x, w_words, w_scales, wgo, offs, out):
         raw_a = [keep.tile([P, PACK, CHUNK], F32, name=f"raw_a{c}") for c in range(2)]
         raw_b = keep.tile([P, PACK, HALF], F32, name="raw_b")
         grouped = [
-            windows.tile([P, HALF, PACK], BF16, name="grouped0", tag="window", align_bytes=64),
+            keep.tile([P, HALF, PACK], BF16, name="grouped0", align_bytes=64),
             keep.tile([P, HALF, PACK], BF16, name="grouped1", align_bytes=64),
         ]
         codes = [keep.tile([P, HALF], U32, name=f"codes{h}", align_bytes=64) for h in range(2)]
@@ -51,14 +51,14 @@ def tile_list_hscat_none_kernel(tc, x, w_words, w_scales, wgo, offs, out):
         nc.gpsimd.memset(w_plane[:].bitcast(I32), 0)
         nc.sync.dma_start(out=raw_a[0][:], in_=x_rows[:, :, 0:CHUNK])
         nc.sync.dma_start(out=raw_a[1][:], in_=x_rows[:, :, CHUNK : 2 * CHUNK])
-        nc.scalar.dma_start(out=words[:].bitcast(I32), in_=w_words[0].bitcast(I32))
         for q in range(4):
             nc.scalar.dma_start(
                 out=w_plane[32 * q : 32 * q + 4, :].bitcast(I32),
                 in_=w_scales[0, 4 * q : 4 * q + 4, :].bitcast(I32),
             )
-        nc.sync.dma_start(offsets[:], offs)
+        nc.scalar.dma_start(out=words[:].bitcast(I32), in_=w_words[0].bitcast(I32))
         nc.sync.dma_start(out=weights[0][:], in_=wgo[:, 0:HALF])
+        nc.sync.dma_start(offsets[:], offs)
         nc.sync.dma_start(out=raw_b[:], in_=x_rows[:, :, HALF:S])
         nc.sync.dma_start(out=weights[1][:], in_=wgo[:, HALF:S])
 
@@ -103,6 +103,7 @@ def tile_list_hscat_none_kernel(tc, x, w_words, w_scales, wgo, offs, out):
 
         clear(0)
         clear(1)
+        clear(2)
 
         group(nc.vector.tensor_copy, 0, raw_a[0], 0, 0, CHUNK)
         quantize(0, 0, CHUNK)
@@ -112,7 +113,6 @@ def tile_list_hscat_none_kernel(tc, x, w_words, w_scales, wgo, offs, out):
         quantize(0, CHUNK, HALF)
         multiply(0, 0, CHUNK, HALF)
         multiply(1, 0, 0, HALF)
-        clear(2)
         place(0, 0)
         group(nc.scalar.copy, 1, raw_b, 0, 0, HALF)
         place(1, 0)

@@ -16,121 +16,116 @@ FP4X4 = mybir.dt.float4_e2m1fn_x4
 
 P = 128
 PACK = 4
-HALF = 512
-CHUNK = 256
 BLOCKS = M // P
+HALF = S // 2
 LIST_COLS = HALF // 16
+CHUNK = HALF // 2
 VECTOR_COLS = 160
+WINDOWS = 3
 
 
 def tile_list_hscat_none_kernel(tc, x, w_words, w_scales, wgo, offs, out):
     nc = tc.nc
-    mult = mybir.AluOpType.mult
-    x_rows = x.rearrange("(p j) s -> p j s", j=PACK)
+    x_rows = x.rearrange("(p i) j -> p i j", i=PACK)
 
     with ExitStack() as ctx:
         keep = ctx.enter_context(tc.tile_pool(name="keep", bufs=1))
-        windows = ctx.enter_context(tc.tile_pool(name="windows", bufs=3))
+        window_pool = ctx.enter_context(tc.tile_pool(name="window_pool", bufs=WINDOWS))
         psum = ctx.enter_context(tc.psum_pool(name="psum", bufs=1))
 
         offsets = keep.tile([P, S // 16], U16, name="offsets")
         words = keep.tile([P, 2 * M], U8, name="words", align_bytes=64)
         w_plane = keep.tile([P, M], U8, name="w_plane", align_bytes=64)
-        weights = [keep.tile([P, HALF], F32, name=f"weights{h}") for h in range(2)]
-        raw_a = [keep.tile([P, PACK, CHUNK], F32, name=f"raw_a{c}") for c in range(2)]
-        raw_b = keep.tile([P, PACK, HALF], F32, name="raw_b")
-        grouped = [
-            keep.tile([P, HALF, PACK], BF16, name="grouped0", align_bytes=64),
-            keep.tile([P, HALF, PACK], BF16, name="grouped1", align_bytes=64),
-        ]
+        out_weights = [keep.tile([P, HALF], F32, name=f"out_weights{h}") for h in range(2)]
+        raw_chunks = [keep.tile([P, PACK, CHUNK], F32, name=f"raw_chunk{c}") for c in range(2)]
+        raw_second = keep.tile([P, PACK, HALF], F32, name="raw_second", tag="shared")
+        grouped = [keep.tile([P, HALF, PACK], BF16, name=f"grouped{h}", align_bytes=64) for h in range(2)]
         codes = [keep.tile([P, HALF], U32, name=f"codes{h}", align_bytes=64) for h in range(2)]
         x_plane = [keep.tile([P, HALF], U8, name=f"x_plane{h}", align_bytes=64) for h in range(2)]
-        result = [[keep.tile([P, HALF], F32, name=f"result{b}{h}") for h in range(2)] for b in range(BLOCKS)]
-        bank = [[psum.tile([P, HALF], F32, name=f"bank{b}{h}") for h in range(2)] for b in range(BLOCKS)]
+        banks = [[psum.tile([P, HALF], F32, name=f"bank{b}{h}") for h in range(2)] for b in range(BLOCKS)]
+        products = {}
+        windows = {}
 
         nc.gpsimd.memset(w_plane[:].bitcast(I32), 0)
-        nc.sync.dma_start(out=raw_a[0][:], in_=x_rows[:, :, 0:CHUNK])
-        nc.sync.dma_start(out=raw_a[1][:], in_=x_rows[:, :, CHUNK : 2 * CHUNK])
+        nc.sync.dma_start(offsets[:], offs)
+        for c in range(2):
+            nc.sync.dma_start(out=raw_chunks[c][:], in_=x_rows[:, :, CHUNK * c : CHUNK * (c + 1)])
         for q in range(4):
             nc.scalar.dma_start(
                 out=w_plane[32 * q : 32 * q + 4, :].bitcast(I32),
                 in_=w_scales[0, 4 * q : 4 * q + 4, :].bitcast(I32),
             )
-        nc.scalar.dma_start(out=words[:].bitcast(I32), in_=w_words[0].bitcast(I32))
-        nc.sync.dma_start(out=weights[0][:], in_=wgo[:, 0:HALF])
-        nc.sync.dma_start(offsets[:], offs)
-        nc.sync.dma_start(out=raw_b[:], in_=x_rows[:, :, HALF:S])
-        nc.sync.dma_start(out=weights[1][:], in_=wgo[:, HALF:S])
+        nc.sync.dma_start(out=words[:].bitcast(I32), in_=w_words[0].bitcast(I32))
+        nc.sync.dma_start(out=out_weights[0][:], in_=wgo[:, 0:HALF])
+        nc.sync.dma_start(out=raw_second[:], in_=x_rows[:, :, HALF:S])
+        nc.sync.dma_start(out=out_weights[1][:], in_=wgo[:, HALF:S])
 
-        window = {}
-
-        def clear(b):
-            window[b] = windows.tile([P, T], F32, name=f"window{b}", tag="window", align_bytes=64)
-            nc.vector.memset(window[b][:], 0.0)
-
-        def group(engine_copy, h, src, first, c0, c1):
-            engine_copy(out=grouped[h][:, c0:c1, :], in_=src[:, :, c0 - first : c1 - first].rearrange("p j c -> p c j"))
-
-        def quantize(h, c0, c1):
-            nc.vector.quantize_mx(
-                out=codes[h][:, c0:c1].bitcast(FP8X4),
-                scales=x_plane[h][:, c0:c1],
-                in_=grouped[h][:, c0:c1, :].rearrange("p c j -> p (c j)"),
+        def group(engine_copy, raw, raw_c0, half, c0, c1):
+            engine_copy(
+                out=grouped[half][:, c0:c1, :],
+                in_=raw[:, :, c0 - raw_c0 : c1 - raw_c0].rearrange("p i j -> p j i"),
             )
 
-        def multiply(b, h, c0, c1):
+        def quantize(half, c0, c1):
+            nc.vector.quantize_mx(
+                out=codes[half][:, c0:c1].bitcast(FP8X4),
+                scales=x_plane[half][:, c0:c1],
+                in_=grouped[half][:, c0:c1, :].rearrange("p j i -> p (j i)"),
+            )
+
+        def multiply(b, half, c0, c1):
             nc.tensor.matmul_mx(
-                out=bank[b][h][:, c0:c1],
+                out=banks[b][half][:, c0:c1],
                 lhsT=words[:, 2 * P * b : 2 * P * (b + 1)].bitcast(FP4X4),
                 lhsT_scale=w_plane[:, P * b : P * (b + 1)],
-                rhs=codes[h][:, c0:c1].bitcast(FP8X4),
-                rhs_scale=x_plane[h][:, c0:c1],
+                rhs=codes[half][:, c0:c1].bitcast(FP8X4),
+                rhs_scale=x_plane[half][:, c0:c1],
                 start=True,
                 stop=True,
             )
-            nc.scalar.copy(out=result[b][h][:, c0:c1], in_=bank[b][h][:, c0:c1])
+            if c0 == 0:
+                tag = "shared" if (b, half) == (2, 0) else f"product{b}{half}"
+                products[b, half] = keep.tile([P, HALF], F32, name=f"product{b}{half}", tag=tag)
+            nc.scalar.copy(out=products[b, half][:, c0:c1], in_=banks[b][half][:, c0:c1])
 
-        def place(b, h):
+        def place(b, half):
             nc.vector.tensor_tensor(
-                window[b][:].indirect(offsets[:, LIST_COLS * h : LIST_COLS * (h + 1)]),
-                result[b][h][:],
-                weights[h][:],
-                mult,
+                windows[b][:].indirect(offsets[:, LIST_COLS * half : LIST_COLS * (half + 1)]),
+                products[b, half][:],
+                out_weights[half][:],
+                mybir.AluOpType.mult,
             )
 
         def store(b):
-            nc.sync.dma_start(out=out[P * b : P * (b + 1), :], in_=window[b][:])
+            nc.sync.dma_start(out=out[P * b : P * (b + 1), :], in_=windows[b][:])
 
-        clear(0)
-        clear(1)
-        clear(2)
+        for b in range(WINDOWS):
+            windows[b] = window_pool.tile([P, T], F32, name=f"window{b}", tag="window", align_bytes=64)
+            nc.vector.memset(windows[b][:], 0.0)
 
-        group(nc.vector.tensor_copy, 0, raw_a[0], 0, 0, CHUNK)
-        quantize(0, 0, CHUNK)
-        group(nc.vector.tensor_copy, 0, raw_a[1], CHUNK, CHUNK, CHUNK + VECTOR_COLS)
-        group(nc.scalar.copy, 0, raw_a[1], CHUNK, CHUNK + VECTOR_COLS, HALF)
-        multiply(0, 0, 0, CHUNK)
-        quantize(0, CHUNK, HALF)
-        multiply(0, 0, CHUNK, HALF)
+        for c in range(2):
+            c0, c1 = CHUNK * c, CHUNK * (c + 1)
+            group(nc.vector.tensor_copy, raw_chunks[c], c0, 0, c0, c0 + VECTOR_COLS)
+            group(nc.scalar.copy, raw_chunks[c], c0, 0, c0 + VECTOR_COLS, c1)
+            quantize(0, c0, c1)
+        for c in range(2):
+            multiply(0, 0, CHUNK * c, CHUNK * (c + 1))
         multiply(1, 0, 0, HALF)
         place(0, 0)
-        group(nc.scalar.copy, 1, raw_b, 0, 0, HALF)
-        place(1, 0)
-        quantize(1, 0, HALF)
-        multiply(0, 1, 0, HALF)
+
+        group(nc.scalar.copy, raw_second, 0, 1, 0, HALF)
         multiply(2, 0, 0, HALF)
-        multiply(1, 1, 0, HALF)
-        multiply(2, 1, 0, HALF)
+        place(1, 0)
         multiply(3, 0, 0, HALF)
-        multiply(3, 1, 0, HALF)
-        place(0, 1)
-        store(0)
+        quantize(1, 0, HALF)
+        for b in range(BLOCKS):
+            multiply(b, 1, 0, HALF)
         place(2, 0)
-        place(1, 1)
-        store(1)
-        window[3] = window[0]
-        place(3, 0)
-        place(2, 1)
-        store(2)
-        place(3, 1)
+        for b in range(WINDOWS):
+            place(b, 1)
+            store(b)
+
+        windows[3] = windows[0]
+        for half in range(2):
+            place(3, half)
         store(3)

from contextlib import ExitStack

import concourse.mybir as mybir

K, M, T, S = 512, 512, 2048, 1024
FLOPS = 2 * K * M * S

F32 = mybir.dt.float32
BF16 = mybir.dt.bfloat16
I32 = mybir.dt.int32
U32 = mybir.dt.uint32
U16 = mybir.dt.uint16
U8 = mybir.dt.uint8
FP8X4 = mybir.dt.float8_e4m3fn_x4
FP4X4 = mybir.dt.float4_e2m1fn_x4

P = 128
PACK = 4
BLOCKS = M // P
HALF = S // 2
LIST_COLS = HALF // 16
CHUNK = HALF // 2
VECTOR_COLS = 160
WINDOWS = 3


def tile_list_hscat_none_kernel(tc, x, w_words, w_scales, wgo, offs, out):
    nc = tc.nc
    x_rows = x.rearrange("(p i) j -> p i j", i=PACK)

    with ExitStack() as ctx:
        keep = ctx.enter_context(tc.tile_pool(name="keep", bufs=1))
        window_pool = ctx.enter_context(tc.tile_pool(name="window_pool", bufs=WINDOWS))
        psum = ctx.enter_context(tc.psum_pool(name="psum", bufs=1))

        offsets = keep.tile([P, S // 16], U16, name="offsets")
        words = keep.tile([P, 2 * M], U8, name="words", align_bytes=64)
        w_plane = keep.tile([P, M], U8, name="w_plane", align_bytes=64)
        out_weights = [keep.tile([P, HALF], F32, name=f"out_weights{h}") for h in range(2)]
        raw_chunks = [keep.tile([P, PACK, CHUNK], F32, name=f"raw_chunk{c}") for c in range(2)]
        raw_second = keep.tile([P, PACK, HALF], F32, name="raw_second", tag="shared")
        grouped = [keep.tile([P, HALF, PACK], BF16, name=f"grouped{h}", align_bytes=64) for h in range(2)]
        codes = [keep.tile([P, HALF], U32, name=f"codes{h}", align_bytes=64) for h in range(2)]
        x_plane = [keep.tile([P, HALF], U8, name=f"x_plane{h}", align_bytes=64) for h in range(2)]
        banks = [[psum.tile([P, HALF], F32, name=f"bank{b}{h}") for h in range(2)] for b in range(BLOCKS)]
        products = {}
        windows = {}

        nc.gpsimd.memset(w_plane[:].bitcast(I32), 0)
        nc.sync.dma_start(offsets[:], offs)
        for c in range(2):
            nc.sync.dma_start(out=raw_chunks[c][:], in_=x_rows[:, :, CHUNK * c : CHUNK * (c + 1)])
        for q in range(4):
            nc.scalar.dma_start(
                out=w_plane[32 * q : 32 * q + 4, :].bitcast(I32),
                in_=w_scales[0, 4 * q : 4 * q + 4, :].bitcast(I32),
            )
        nc.sync.dma_start(out=words[:].bitcast(I32), in_=w_words[0].bitcast(I32))
        nc.sync.dma_start(out=out_weights[0][:], in_=wgo[:, 0:HALF])
        nc.sync.dma_start(out=raw_second[:], in_=x_rows[:, :, HALF:S])
        nc.sync.dma_start(out=out_weights[1][:], in_=wgo[:, HALF:S])

        def group(engine_copy, raw, raw_c0, half, c0, c1):
            engine_copy(
                out=grouped[half][:, c0:c1, :],
                in_=raw[:, :, c0 - raw_c0 : c1 - raw_c0].rearrange("p i j -> p j i"),
            )

        def quantize(half, c0, c1):
            nc.vector.quantize_mx(
                out=codes[half][:, c0:c1].bitcast(FP8X4),
                scales=x_plane[half][:, c0:c1],
                in_=grouped[half][:, c0:c1, :].rearrange("p j i -> p (j i)"),
            )

        def multiply(b, half, c0, c1):
            nc.tensor.matmul_mx(
                out=banks[b][half][:, c0:c1],
                lhsT=words[:, 2 * P * b : 2 * P * (b + 1)].bitcast(FP4X4),
                lhsT_scale=w_plane[:, P * b : P * (b + 1)],
                rhs=codes[half][:, c0:c1].bitcast(FP8X4),
                rhs_scale=x_plane[half][:, c0:c1],
                start=True,
                stop=True,
            )
            if c0 == 0:
                tag = "shared" if (b, half) == (2, 0) else f"product{b}{half}"
                products[b, half] = keep.tile([P, HALF], F32, name=f"product{b}{half}", tag=tag)
            nc.scalar.copy(out=products[b, half][:, c0:c1], in_=banks[b][half][:, c0:c1])

        def place(b, half):
            nc.vector.tensor_tensor(
                windows[b][:].indirect(offsets[:, LIST_COLS * half : LIST_COLS * (half + 1)]),
                products[b, half][:],
                out_weights[half][:],
                mybir.AluOpType.mult,
            )

        def store(b):
            nc.sync.dma_start(out=out[P * b : P * (b + 1), :], in_=windows[b][:])

        for b in range(WINDOWS):
            windows[b] = window_pool.tile([P, T], F32, name=f"window{b}", tag="window", align_bytes=64)
            nc.vector.memset(windows[b][:], 0.0)

        for c in range(2):
            c0, c1 = CHUNK * c, CHUNK * (c + 1)
            group(nc.vector.tensor_copy, raw_chunks[c], c0, 0, c0, c0 + VECTOR_COLS)
            group(nc.scalar.copy, raw_chunks[c], c0, 0, c0 + VECTOR_COLS, c1)
            quantize(0, c0, c1)
        for c in range(2):
            multiply(0, 0, CHUNK * c, CHUNK * (c + 1))
        multiply(1, 0, 0, HALF)
        place(0, 0)

        group(nc.scalar.copy, raw_second, 0, 1, 0, HALF)
        multiply(2, 0, 0, HALF)
        place(1, 0)
        multiply(3, 0, 0, HALF)
        quantize(1, 0, HALF)
        for b in range(BLOCKS):
            multiply(b, 1, 0, HALF)
        place(2, 0)
        for b in range(WINDOWS):
            place(b, 1)
            store(b)

        windows[3] = windows[0]
        for half in range(2):
            place(3, half)
        store(3)
